import numpy as np
import ml_dtypes


def mxq(x, axis, fmt="e4m3"):
    dtype, down = {"e4m3": (ml_dtypes.float8_e4m3fn, 7), "e5m2": (ml_dtypes.float8_e5m2, 14)}[fmt]
    v = np.moveaxis(np.asarray(x, np.float32).astype(ml_dtypes.bfloat16).astype(np.float64), axis, -1)
    blocks = v.reshape(v.shape[:-1] + (-1, 32))
    amax = np.abs(blocks).max(-1, keepdims=True)
    byte = np.maximum(np.where(amax > 0, np.frexp(amax)[1] - 1 + 127, 0) - down, 1)
    scale = np.exp2(byte - 127.0)
    codes = (blocks / scale).astype(np.float32).astype(dtype).astype(np.float64)
    return np.moveaxis((codes * scale).reshape(v.shape), -1, axis)


WIDE = False


def mx_kscale(k):
    if not WIDE:
        return np.ones(k)
    levels = np.array([10, -10, 5, -5, 0])
    if k % 512:
        return np.exp2(np.random.permutation(np.resize(levels, k // 32))).repeat(32)
    a = np.empty((k // 512, 16))
    for p in range(k // 512):
        a[p, :8] = np.random.permutation(np.resize(levels, 8))
        for g in range(8):
            far = levels[np.abs(levels - a[p, g]) >= 10]
            a[p, g + 8] = far[np.random.randint(len(far))]
    return np.exp2(a.ravel()).repeat(32)


def f64(x):
    return np.asarray(x).astype(np.float64)


def striped(idx):
    return np.tile(np.asarray(idx).reshape(-1, 16).T, (8, 1)).astype(np.uint16)


def unstriped(offs):
    return offs[:16].T.reshape(-1).astype(np.int64)


E2M1 = np.array([0.0, 0.5, 1.0, 1.5, 2.0, 3.0, 4.0, 6.0, -0.0, -0.5, -1.0, -1.5, -2.0, -3.0, -4.0, -6.0])


def pack_weight(w, fmt):
    k, n = w.shape
    w = f64(np.asarray(w, np.float32).astype(ml_dtypes.bfloat16)).reshape(k // 32, 32, n)
    amax = np.abs(w).max(1)
    if fmt == "e4m3":
        byte = np.frexp(amax)[1] - 1 + 127 - 7
    else:
        mant, ex = np.frexp(amax / 6.0)
        byte = np.where(mant > 0.5, ex, ex - 1) + 127
    byte = np.clip(np.where(amax > 0, byte, 1), 1, 254)
    scaled = (w * np.exp2(127.0 - byte)[:, None, :]).reshape(k, n).astype(np.float32)
    by_word = np.ascontiguousarray(scaled.reshape(k // 512, 128, 4, n).transpose(0, 1, 3, 2))
    if fmt == "e4m3":
        words = by_word.astype(ml_dtypes.float8_e4m3fn).view(np.uint8)
    else:
        c = by_word.astype(ml_dtypes.float4_e2m1fn).view(np.uint8) & 0xF
        words = (c[..., 0::2] | (c[..., 1::2] << 4)).reshape(k // 512, 128, 2 * n)
    return np.ascontiguousarray(words), np.ascontiguousarray(byte.astype(np.uint8).reshape(k // 512, 16, n))


def unpack_weight(words, scales, fmt):
    g, _, n = scales.shape
    words = np.ascontiguousarray(words).reshape(g, 128, n, -1)
    if fmt == "e4m3":
        vals = words.view(ml_dtypes.float8_e4m3fn).astype(np.float64)
    else:
        nib = np.empty((g, 128, n, 4), np.uint8)
        nib[..., 0::2] = words & 0xF
        nib[..., 1::2] = words >> 4
        vals = E2M1[nib]
    vals = vals * np.repeat(np.exp2(scales.astype(np.float64) - 127.0), 8, axis=1)[..., None]
    return vals.transpose(0, 1, 3, 2).reshape(g * 512, n)


def sigmoid(v):
    return 1.0 / (1.0 + np.exp(-v))


K, R, F, T, J, U = 512, 128, 512, 2048, 512, 1024


def setup_inputs():
    n = np.random.standard_normal
    idx = np.random.permutation(T)[:J]
    idx2 = np.random.permutation(U)[:J]
    fk = mx_kscale(K)
    ff = mx_kscale(F)
    tabp = pack_weight(n((K, T)) / fk[:, None], "e2m1")
    return {
        "tab_words": tabp[0],
        "tab_scales": tabp[1],
        "w1": (n((K, R)) * 1 / np.sqrt(K) * fk[:, None]).astype(np.float32),
        "w2": (n((K, R)) * 1 / np.sqrt(K) * fk[:, None]).astype(np.float32),
        "bias": (np.random.uniform(-0.5, 0.5, (R, 1))).astype(np.float32),
        "carry": (n((R, U)) * 0.7).astype(np.float32),
        "wo": (n((F, R)) * 1 / np.sqrt(F) * ff[:, None]).astype(np.float32),
        "dy": (n((F, J)) / ff[:, None]).astype(np.float32),
        "og": (np.random.uniform(0.3, 1.0, (R, 1))).astype(np.float32),
        "base": (0.3 * n((R, J))).astype(np.float32),
        "offs": striped(idx),
        "offs2": striped(idx2),
    }


def reference(tab_words, tab_scales, w1, w2, bias, carry, wo, dy, og, base, offs, offs2):
    idx = unstriped(offs)
    idx2 = unstriped(offs2)
    tabu = unpack_weight(tab_words, tab_scales, "e2m1")
    w1q = mxq(f64(w1), 0, "e4m3")
    tabidxg = tabu[:, idx]
    a = w1q.T @ tabidxg
    w2q = mxq(f64(w2), 0, "e4m3")
    b = w2q.T @ tabidxg
    h1 = np.tanh(a)
    gt = sigmoid(b + f64(bias))
    woq = mxq(f64(wo), 0, "e4m3")
    dyq = mxq(f64(dy), 0, "e4m3")
    c0 = woq.T @ dyq
    dgt = c0 * (h1 - f64(carry)[:, idx2])
    db = dgt * gt * (1.0 - gt)
    hdb = db * 2.0
    hgt = hdb * (1.0 - gt) * dgt - hdb * dgt * gt
    hb = hgt * gt * (1.0 - gt)
    y = hb * f64(og) + f64(base)
    return y

@@ -1,0 +1,139 @@
+import math
+from contextlib import ExitStack
+
+import concourse.mybir as mybir
+
+K, R, F, T, J, U = 512, 128, 512, 2048, 512, 1024
+FLOPS = 3 * 2 * K * R * J
+
+F32 = mybir.dt.float32
+BF16 = mybir.dt.bfloat16
+I32 = mybir.dt.int32
+U32 = mybir.dt.uint32
+U16 = mybir.dt.uint16
+U8 = mybir.dt.uint8
+FP8X4 = mybir.dt.float8_e4m3fn_x4
+FP4X4 = mybir.dt.float4_e2m1fn_x4
+ACT = mybir.ActivationFunctionType
+ALU = mybir.AluOpType
+
+P = 128
+PACK = 4
+HALVES = 2
+JH = J // HALVES
+
+
+def interleave(copy, grouped, raw):
+    copy(
+        out=grouped.rearrange("p (c i) t -> p c t i", i=4),
+        in_=raw.rearrange("p t (c i) -> p c t i", i=4),
+    )
+
+
+def quantise(nc, codes, scales, grouped):
+    nc.vector.quantize_mx(out=codes.bitcast(FP8X4), scales=scales, in_=grouped.rearrange("p c t -> p (c t)"))
+
+
+def tile_attend_gpcarrymix_kernel(tc, tab_words, tab_scales, w1, w2, bias, carry, wo, dy, og, base, offs, offs2, out):
+    nc = tc.nc
+    with ExitStack() as ctx:
+        sb = ctx.enter_context(tc.tile_pool(name="sb", bufs=1))
+        ps = ctx.enter_context(tc.psum_pool(name="ps", bufs=1))
+
+        def tile(name, shape, dtype):
+            return sb.tile(shape, dtype, name=name, align_bytes=64)
+
+        offs_sb = tile("offs_sb", [P, J // 16], U16)
+        offs2_sb = tile("offs2_sb", [P, J // 16], U16)
+        words = tile("words", [P, T], U16)
+        bytes_ = tile("scale_bytes", [P, T], U8)
+        bias_sb = tile("bias_sb", [P, 1], F32)
+        og_sb = tile("og_sb", [P, 1], F32)
+        carry_sb = tile("carry_sb", [P, U], F32)
+        raw = {n: tile(n + "_raw", [P, PACK, R], F32) for n in ("w2", "w1", "wo")}
+        dy_raw = [tile("dy_raw%d" % h, [P, PACK, JH], F32) for h in range(HALVES)]
+        base_sb = tile("base_sb", [P, J], F32)
+
+        nc.vector.memset(bytes_[:].bitcast(I32), 0)
+        nc.gpsimd.dma_start(out=bias_sb[:], in_=bias)
+        nc.gpsimd.dma_start(out=og_sb[:], in_=og)
+        nc.sync.dma_start(offs_sb[:], offs)
+        for q in range(4):
+            nc.scalar.dma_start(
+                out=bytes_[32 * q : 32 * q + 4, :].bitcast(I32),
+                in_=tab_scales[0, 4 * q : 4 * q + 4, :].bitcast(I32),
+            )
+        nc.sync.dma_start(out=words[:].bitcast(I32), in_=tab_words[0].bitcast(I32))
+        nc.sync.dma_start(out=raw["w2"][:], in_=w2.rearrange("(p t) r -> p t r", t=PACK))
+        nc.sync.dma_start(out=raw["w1"][:], in_=w1.rearrange("(p t) r -> p t r", t=PACK))
+        nc.sync.dma_start(offs2_sb[:], offs2)
+        nc.sync.dma_start(out=carry_sb[:], in_=carry)
+        nc.sync.dma_start(out=raw["wo"][:], in_=wo.rearrange("(p t) r -> p t r", t=PACK))
+        dy_v = dy.rearrange("(p t) j -> p t j", t=PACK)
+        for h in range(HALVES):
+            nc.sync.dma_start(out=dy_raw[h][:], in_=dy_v[:, :, h * JH : (h + 1) * JH])
+        nc.sync.dma_start(out=base_sb[:], in_=base)
+
+        half_bias = tile("half_bias", [P, 1], F32)
+        nc.scalar.activation(out=half_bias[:], in_=bias_sb[:], func=ACT.Copy, scale=0.5)
+
+        g_bytes = tile("g_bytes", [P, J], U8)
+        g_words = tile("g_words", [P, J], U16)
+        nc.vector.tensor_copy(g_bytes[:], bytes_[:].indirect(offs_sb[:]))
+        nc.vector.tensor_copy(g_words[:], words[:].indirect(offs_sb[:]))
+
+        grouped, codes, scales = {}, {}, {}
+        for n in ("w2", "w1", "wo"):
+            grouped[n] = tile(n + "_grouped", [P, R, PACK], BF16)
+            codes[n] = tile(n + "_codes", [P, R], U32)
+            scales[n] = tile(n + "_scales", [P, R], U8)
+
+        sums = {}
+        for n in ("w2", "w1"):
+            interleave(nc.scalar.copy, grouped[n][:], raw[n][:])
+            quantise(nc, codes[n][:], scales[n][:], grouped[n][:])
+            sums[n] = ps.tile([P, J], F32, name=n + "_sums")
+            nc.tensor.matmul_mx(
+                out=sums[n][:], lhsT=codes[n][:].bitcast(FP8X4), lhsT_scale=scales[n][:],
+                rhs=g_words[:].bitcast(FP4X4), rhs_scale=g_bytes[:], start=True, stop=True,
+            )
+
+        g_carry = tile("g_carry", [P, J], F32)
+        nc.vector.tensor_copy(g_carry[:], carry_sb[:].indirect(offs2_sb[:]))
+
+        t = tile("t", [P, J], F32)
+        h1 = tile("h1", [P, J], F32)
+        t2 = tile("t2", [P, J], F32)
+        nc.scalar.activation(out=t[:], in_=sums["w2"][:], func=ACT.Tanh, bias=half_bias[:], scale=0.5)
+        nc.scalar.activation(out=h1[:], in_=sums["w1"][:], func=ACT.Tanh)
+        nc.scalar.activation(out=t2[:], in_=t[:], func=ACT.Square)
+
+        interleave(nc.vector.tensor_copy, grouped["wo"][:], raw["wo"][:])
+        d = tile("d", [P, J], F32)
+        e = tile("e", [P, J], F32)
+        nc.vector.tensor_tensor(d[:], h1[:], g_carry[:], ALU.subtract)
+        quantise(nc, codes["wo"][:], scales["wo"][:], grouped["wo"][:])
+        nc.vector.scalar_tensor_tensor(e[:], t2[:], 1.0, d[:], ALU.subtract, ALU.mult)
+
+        c0, q, q2, r, y = [], [], [], [], []
+        for h in range(HALVES):
+            dy_grouped = tile("dy_grouped%d" % h, [P, JH, PACK], BF16)
+            dy_codes = tile("dy_codes%d" % h, [P, JH], U32)
+            dy_scales = tile("dy_scales%d" % h, [P, JH], U8)
+            interleave(nc.scalar.copy if h == 0 else nc.vector.tensor_copy, dy_grouped[:], dy_raw[h][:])
+            quantise(nc, dy_codes[:], dy_scales[:], dy_grouped[:])
+            c0.append(ps.tile([P, JH], F32, name="c0_%d" % h))
+            nc.tensor.matmul_mx(
+                out=c0[h][:], lhsT=codes["wo"][:].bitcast(FP8X4), lhsT_scale=scales["wo"][:],
+                rhs=dy_codes[:].bitcast(FP8X4), rhs_scale=dy_scales[:], start=True, stop=True,
+            )
+            for lst, n in ((q, "q"), (q2, "q2"), (r, "r"), (y, "y")):
+                lst.append(tile("%s%d" % (n, h), [P, JH], F32))
+
+        for h in range(HALVES):
+            cols = slice(h * JH, (h + 1) * JH)
+            nc.vector.tensor_tensor(q[h][:], c0[h][:], e[:, cols], ALU.mult)
+            nc.scalar.activation(out=q2[h][:], in_=q[h][:], func=ACT.Square, scale=math.sqrt(0.125))
+            nc.vector.scalar_tensor_tensor(r[h][:], q2[h][:], og_sb[:], t[:, cols], ALU.mult, ALU.mult)
+            nc.vector.tensor_tensor(y[h][:], base_sb[:, cols], r[h][:], ALU.subtract)
+            nc.sync.dma_start(out=out[:, cols], in_=y[h][:])

@@ -21,6 +21,7 @@ P = 128
 PACK = 4
 HALVES = 2
 JH = J // HALVES
+SCALAR_COLS = [256,96]
 
 
 def interleave(copy, grouped, raw):
@@ -40,8 +41,11 @@ def tile_attend_gpcarrymix_kernel(tc, tab_words, tab_scales, w1, w2, bias, carry
         sb = ctx.enter_context(tc.tile_pool(name="sb", bufs=1))
         ps = ctx.enter_context(tc.psum_pool(name="ps", bufs=1))
 
-        def tile(name, shape, dtype):
-            return sb.tile(shape, dtype, name=name, align_bytes=64)
+        def tile(name, shape, dtype, tag=None):
+            return sb.tile(shape, dtype, name=name, tag=tag or name, align_bytes=64)
+
+        def scalar_cast(out, in_):
+            nc.scalar.activation(out=out, in_=in_, func=ACT.Copy)
 
         offs_sb = tile("offs_sb", [P, J // 16], U16)
         offs2_sb = tile("offs2_sb", [P, J // 16], U16)
@@ -53,87 +57,126 @@ def tile_attend_gpcarrymix_kernel(tc, tab_words, tab_scales, w1, w2, bias, carry
         raw = {n: tile(n + "_raw", [P, PACK, R], F32) for n in ("w2", "w1", "wo")}
         dy_raw = [tile("dy_raw%d" % h, [P, PACK, JH], F32) for h in range(HALVES)]
         base_sb = tile("base_sb", [P, J], F32)
-
-        nc.vector.memset(bytes_[:].bitcast(I32), 0)
-        nc.gpsimd.dma_start(out=bias_sb[:], in_=bias)
-        nc.gpsimd.dma_start(out=og_sb[:], in_=og)
-        nc.sync.dma_start(offs_sb[:], offs)
-        for q in range(4):
-            nc.scalar.dma_start(
-                out=bytes_[32 * q : 32 * q + 4, :].bitcast(I32),
-                in_=tab_scales[0, 4 * q : 4 * q + 4, :].bitcast(I32),
-            )
-        nc.sync.dma_start(out=words[:].bitcast(I32), in_=tab_words[0].bitcast(I32))
-        nc.sync.dma_start(out=raw["w2"][:], in_=w2.rearrange("(p t) r -> p t r", t=PACK))
-        nc.sync.dma_start(out=raw["w1"][:], in_=w1.rearrange("(p t) r -> p t r", t=PACK))
-        nc.sync.dma_start(offs2_sb[:], offs2)
-        nc.sync.dma_start(out=carry_sb[:], in_=carry)
-        nc.sync.dma_start(out=raw["wo"][:], in_=wo.rearrange("(p t) r -> p t r", t=PACK))
         dy_v = dy.rearrange("(p t) j -> p t j", t=PACK)
-        for h in range(HALVES):
-            nc.sync.dma_start(out=dy_raw[h][:], in_=dy_v[:, :, h * JH : (h + 1) * JH])
-        nc.sync.dma_start(out=base_sb[:], in_=base)
+        weights = {"w2": w2, "w1": w1, "wo": wo}
 
-        half_bias = tile("half_bias", [P, 1], F32)
-        nc.scalar.activation(out=half_bias[:], in_=bias_sb[:], func=ACT.Copy, scale=0.5)
+        def load(name, eng):
+            if name == "scales":
+                for q in range(4):
+                    eng.dma_start(
+                        out=bytes_[32 * q : 32 * q + 4, :].bitcast(I32),
+                        in_=tab_scales[0, 4 * q : 4 * q + 4, :].bitcast(I32),
+                    )
+            elif name in weights:
+                eng.dma_start(out=raw[name][:], in_=weights[name].rearrange("(p t) r -> p t r", t=PACK))
+            elif name == "words":
+                eng.dma_start(out=words[:].bitcast(I32), in_=tab_words[0].bitcast(I32))
+            elif name in ("dy0", "dy1"):
+                h = int(name[2])
+                eng.dma_start(out=dy_raw[h][:], in_=dy_v[:, :, h * JH : (h + 1) * JH])
+            else:
+                dst, src = {"offs": (offs_sb, offs), "offs2": (offs2_sb, offs2), "bias": (bias_sb, bias), "og": (og_sb, og),
+                            "carry": (carry_sb, carry), "base": (base_sb, base)}[name]
+                eng.dma_start(dst[:], src)
+
+        nc.vector.memset(bytes_[:].bitcast(I32)[:, :256], 0)
+        nc.gpsimd.memset(bytes_[:].bitcast(I32)[:, 256:], 0)
+        load("og", nc.gpsimd)
+        load("offs", nc.sync)
+        load("bias", nc.sync)
+        load("words", nc.sync)
+        load("scales", nc.sync)
+        load("w1", nc.sync)
+        load("w2", nc.sync)
+        load("wo", nc.sync)
+        load("dy0", nc.sync)
+        load("carry", nc.sync)
+        load("offs2", nc.sync)
+        load("dy1", nc.sync)
+        load("base", nc.sync)
 
         g_bytes = tile("g_bytes", [P, J], U8)
         g_words = tile("g_words", [P, J], U16)
-        nc.vector.tensor_copy(g_bytes[:], bytes_[:].indirect(offs_sb[:]))
-        nc.vector.tensor_copy(g_words[:], words[:].indirect(offs_sb[:]))
 
-        grouped, codes, scales = {}, {}, {}
-        for n in ("w2", "w1", "wo"):
-            grouped[n] = tile(n + "_grouped", [P, R, PACK], BF16)
-            codes[n] = tile(n + "_codes", [P, R], U32)
-            scales[n] = tile(n + "_scales", [P, R], U8)
+        pair_grouped = tile("pair_grouped", [P, 2 * R, PACK], BF16)
+        pair_codes = tile("pair_codes", [P, 2 * R], U32)
+        pair_scales = tile("pair_scales", [P, 2 * R], U8)
+        grouped = {"wo": tile("wo_grouped", [P, R, PACK], BF16)}
+        codes = {"wo": tile("wo_codes", [P, R], U32)}
+        scales = {"wo": tile("wo_scales", [P, R], U8)}
+        part = {"w1": slice(0, R), "w2": slice(R, 2 * R)}
+        for n in part:
+            interleave(scalar_cast, pair_grouped[:, part[n], :], raw[n][:])
+        interleave(scalar_cast, grouped["wo"][:], raw["wo"][:])
+        half_bias = tile("half_bias", [P, 1], F32)
+        nc.scalar.activation(out=half_bias[:], in_=bias_sb[:], func=ACT.Copy, scale=0.5)
 
-        sums = {}
-        for n in ("w2", "w1"):
-            interleave(nc.scalar.copy, grouped[n][:], raw[n][:])
-            quantise(nc, codes[n][:], scales[n][:], grouped[n][:])
-            sums[n] = ps.tile([P, J], F32, name=n + "_sums")
-            nc.tensor.matmul_mx(
-                out=sums[n][:], lhsT=codes[n][:].bitcast(FP8X4), lhsT_scale=scales[n][:],
-                rhs=g_words[:].bitcast(FP4X4), rhs_scale=g_bytes[:], start=True, stop=True,
-            )
-
-        g_carry = tile("g_carry", [P, J], F32)
-        nc.vector.tensor_copy(g_carry[:], carry_sb[:].indirect(offs2_sb[:]))
-
+        cols = [slice(h * JH, (h + 1) * JH) for h in range(HALVES)]
+        ocols = [slice(h * JH // 16, (h + 1) * JH // 16) for h in range(HALVES)]
         t = tile("t", [P, J], F32)
         h1 = tile("h1", [P, J], F32)
         t2 = tile("t2", [P, J], F32)
-        nc.scalar.activation(out=t[:], in_=sums["w2"][:], func=ACT.Tanh, bias=half_bias[:], scale=0.5)
-        nc.scalar.activation(out=h1[:], in_=sums["w1"][:], func=ACT.Tanh)
-        nc.scalar.activation(out=t2[:], in_=t[:], func=ACT.Square)
-
-        interleave(nc.vector.tensor_copy, grouped["wo"][:], raw["wo"][:])
         d = tile("d", [P, J], F32)
         e = tile("e", [P, J], F32)
-        nc.vector.tensor_tensor(d[:], h1[:], g_carry[:], ALU.subtract)
-        quantise(nc, codes["wo"][:], scales["wo"][:], grouped["wo"][:])
-        nc.vector.scalar_tensor_tensor(e[:], t2[:], 1.0, d[:], ALU.subtract, ALU.mult)
 
-        c0, q, q2, r, y = [], [], [], [], []
-        for h in range(HALVES):
-            dy_grouped = tile("dy_grouped%d" % h, [P, JH, PACK], BF16)
-            dy_codes = tile("dy_codes%d" % h, [P, JH], U32)
-            dy_scales = tile("dy_scales%d" % h, [P, JH], U8)
-            interleave(nc.scalar.copy if h == 0 else nc.vector.tensor_copy, dy_grouped[:], dy_raw[h][:])
-            quantise(nc, dy_codes[:], dy_scales[:], dy_grouped[:])
-            c0.append(ps.tile([P, JH], F32, name="c0_%d" % h))
+        nc.vector.tensor_copy(g_words[:], words[:].indirect(offs_sb[:]))
+        nc.vector.tensor_copy(g_bytes[:], bytes_[:].indirect(offs_sb[:]))
+        sums = {}
+        quantise(nc, pair_codes[:], pair_scales[:], pair_grouped[:])
+        for n in ("w1", "w2"):
+            sums[n] = ps.tile([P, J], F32, name=n + "_sums")
             nc.tensor.matmul_mx(
-                out=c0[h][:], lhsT=codes["wo"][:].bitcast(FP8X4), lhsT_scale=scales["wo"][:],
-                rhs=dy_codes[:].bitcast(FP8X4), rhs_scale=dy_scales[:], start=True, stop=True,
+                out=sums[n][:], lhsT=pair_codes[:, part[n]].bitcast(FP8X4), lhsT_scale=pair_scales[:, part[n]],
+                rhs=g_words[:].bitcast(FP4X4), rhs_scale=g_bytes[:], start=True, stop=True,
             )
-            for lst, n in ((q, "q"), (q2, "q2"), (r, "r"), (y, "y")):
-                lst.append(tile("%s%d" % (n, h), [P, JH], F32))
+        nc.scalar.activation(out=h1[:], in_=sums["w1"][:], func=ACT.Tanh)
+        nc.scalar.activation(out=t[:], in_=sums["w2"][:], func=ACT.Tanh, bias=half_bias[:], scale=0.5)
+        nc.scalar.activation(out=t2[:], in_=t[:], func=ACT.Square)
+        quantise(nc, codes["wo"][:], scales["wo"][:], grouped["wo"][:])
 
-        for h in range(HALVES):
-            cols = slice(h * JH, (h + 1) * JH)
-            nc.vector.tensor_tensor(q[h][:], c0[h][:], e[:, cols], ALU.mult)
-            nc.scalar.activation(out=q2[h][:], in_=q[h][:], func=ACT.Square, scale=math.sqrt(0.125))
-            nc.vector.scalar_tensor_tensor(r[h][:], q2[h][:], og_sb[:], t[:, cols], ALU.mult, ALU.mult)
-            nc.vector.tensor_tensor(y[h][:], base_sb[:, cols], r[h][:], ALU.subtract)
-            nc.sync.dma_start(out=out[:, cols], in_=y[h][:])
+        pieces = [(0, 0, 256, nc.vector.tensor_copy), (1, 0, 128, scalar_cast), (1, 128, 128, scalar_cast)]
+        work = []
+        for i, (h, c, w, copy) in enumerate(pieces):
+            names = {"grouped": ([P, w, PACK], BF16), "codes": ([P, w], U32), "scales": ([P, w], U8),
+                     "q": ([P, w], F32), "q2": ([P, w], F32), "r": ([P, w], F32), "y": ([P, w], F32)}
+            x = {n: tile("dy_%s%d" % (n, i), *spec, tag="dy_raw1" if (n, i) == ("q2", 0) else None) for n, spec in names.items()}
+            x["c0"] = ps.tile([P, w], F32, name="c0_%d" % i)
+            x["cols"] = slice(h * JH + c, h * JH + c + w)
+            x["copy"], x["raw"] = copy, dy_raw[h][:, :, c : c + w]
+            work.append(x)
+
+        def lay(x):
+            interleave(x["copy"], x["grouped"][:], x["raw"])
+
+        def product(x):
+            quantise(nc, x["codes"][:], x["scales"][:], x["grouped"][:])
+            nc.tensor.matmul_mx(
+                out=x["c0"][:], lhsT=codes["wo"][:].bitcast(FP8X4), lhsT_scale=scales["wo"][:],
+                rhs=x["codes"][:].bitcast(FP8X4), rhs_scale=x["scales"][:], start=True, stop=True,
+            )
+
+        def square(x):
+            nc.vector.tensor_tensor(x["q"][:], x["c0"][:], e[:, x["cols"]], ALU.mult)
+            nc.scalar.activation(out=x["q2"][:], in_=x["q"][:], func=ACT.Square, scale=math.sqrt(0.125))
+
+        def gain(x):
+            nc.vector.scalar_tensor_tensor(x["r"][:], x["q2"][:], og_sb[:], t[:, x["cols"]], ALU.mult, ALU.mult)
+
+        def finish(x):
+            nc.vector.tensor_tensor(x["y"][:], base_sb[:, x["cols"]], x["r"][:], ALU.subtract)
+            nc.sync.dma_start(out=out[:, x["cols"]], in_=x["y"][:])
+
+        lay(work[0])
+        product(work[0])
+        nc.vector.tensor_tensor(d[:], carry_sb[:].indirect(offs2_sb[:]), h1[:], ALU.subtract)
+        nc.vector.scalar_tensor_tensor(e[:], t2[:], 1.0, d[:], ALU.subtract, ALU.mult)
+        for x in work[1:]:
+            lay(x)
+        square(work[0])
+        for x in work[1:]:
+            product(x)
+        for x in work[1:]:
+            square(x)
+        for x in work:
+            gain(x)
+            finish(x)

@@ -81,17 +81,17 @@ def tile_attend_gpcarrymix_kernel(tc, tab_words, tab_scales, w1, w2, bias, carry
 
         nc.vector.memset(bytes_[:].bitcast(I32)[:, :256], 0)
         nc.gpsimd.memset(bytes_[:].bitcast(I32)[:, 256:], 0)
+        load("bias", nc.gpsimd)
         load("og", nc.gpsimd)
         load("offs", nc.sync)
-        load("bias", nc.sync)
+        load("offs2", nc.sync)
         load("words", nc.sync)
         load("scales", nc.sync)
-        load("w1", nc.sync)
         load("w2", nc.sync)
+        load("w1", nc.sync)
+        load("carry", nc.sync)
         load("wo", nc.sync)
         load("dy0", nc.sync)
-        load("carry", nc.sync)
-        load("offs2", nc.sync)
         load("dy1", nc.sync)
         load("base", nc.sync)
 
@@ -104,12 +104,12 @@ def tile_attend_gpcarrymix_kernel(tc, tab_words, tab_scales, w1, w2, bias, carry
         grouped = {"wo": tile("wo_grouped", [P, R, PACK], BF16)}
         codes = {"wo": tile("wo_codes", [P, R], U32)}
         scales = {"wo": tile("wo_scales", [P, R], U8)}
-        part = {"w1": slice(0, R), "w2": slice(R, 2 * R)}
+        part = {"w2": slice(0, R), "w1": slice(R, 2 * R)}
         for n in part:
             interleave(scalar_cast, pair_grouped[:, part[n], :], raw[n][:])
         interleave(scalar_cast, grouped["wo"][:], raw["wo"][:])
         half_bias = tile("half_bias", [P, 1], F32)
-        nc.scalar.activation(out=half_bias[:], in_=bias_sb[:], func=ACT.Copy, scale=0.5)
+        nc.gpsimd.tensor_scalar(half_bias[:], bias_sb[:], 0.5, 0.0, ALU.mult, ALU.add)
 
         cols = [slice(h * JH, (h + 1) * JH) for h in range(HALVES)]
         ocols = [slice(h * JH // 16, (h + 1) * JH // 16) for h in range(HALVES)]
@@ -123,15 +123,17 @@ def tile_attend_gpcarrymix_kernel(tc, tab_words, tab_scales, w1, w2, bias, carry
         nc.vector.tensor_copy(g_bytes[:], bytes_[:].indirect(offs_sb[:]))
         sums = {}
         quantise(nc, pair_codes[:], pair_scales[:], pair_grouped[:])
-        for n in ("w1", "w2"):
+        for n in ("w2", "w1"):
             sums[n] = ps.tile([P, J], F32, name=n + "_sums")
             nc.tensor.matmul_mx(
                 out=sums[n][:], lhsT=pair_codes[:, part[n]].bitcast(FP8X4), lhsT_scale=pair_scales[:, part[n]],
                 rhs=g_words[:].bitcast(FP4X4), rhs_scale=g_bytes[:], start=True, stop=True,
             )
-        nc.scalar.activation(out=h1[:], in_=sums["w1"][:], func=ACT.Tanh)
         nc.scalar.activation(out=t[:], in_=sums["w2"][:], func=ACT.Tanh, bias=half_bias[:], scale=0.5)
+        nc.scalar.activation(out=h1[:], in_=sums["w1"][:], func=ACT.Tanh)
         nc.scalar.activation(out=t2[:], in_=t[:], func=ACT.Square)
+        g_carry = tile("g_carry", [P, J], F32, tag="pair_grouped")
+        nc.vector.tensor_copy(g_carry[:], carry_sb[:].indirect(offs2_sb[:]))
         quantise(nc, codes["wo"][:], scales["wo"][:], grouped["wo"][:])
 
         pieces = [(0, 0, 256, nc.vector.tensor_copy), (1, 0, 128, scalar_cast), (1, 128, 128, scalar_cast)]
@@ -168,14 +170,13 @@ def tile_attend_gpcarrymix_kernel(tc, tab_words, tab_scales, w1, w2, bias, carry
 
         lay(work[0])
         product(work[0])
-        nc.vector.tensor_tensor(d[:], carry_sb[:].indirect(offs2_sb[:]), h1[:], ALU.subtract)
+        nc.vector.tensor_tensor(d[:], h1[:], g_carry[:], ALU.subtract)
         nc.vector.scalar_tensor_tensor(e[:], t2[:], 1.0, d[:], ALU.subtract, ALU.mult)
         for x in work[1:]:
             lay(x)
-        square(work[0])
         for x in work[1:]:
             product(x)
-        for x in work[1:]:
+        for x in work:
             square(x)
         for x in work:
             gain(x)

import math
from contextlib import ExitStack

import concourse.mybir as mybir

K, R, F, T, J, U = 512, 128, 512, 2048, 512, 1024
FLOPS = 3 * 2 * K * R * J

F32 = mybir.dt.float32
BF16 = mybir.dt.bfloat16
I32 = mybir.dt.int32
U32 = mybir.dt.uint32
U16 = mybir.dt.uint16
U8 = mybir.dt.uint8
FP8X4 = mybir.dt.float8_e4m3fn_x4
FP4X4 = mybir.dt.float4_e2m1fn_x4
ACT = mybir.ActivationFunctionType
ALU = mybir.AluOpType

P = 128
PACK = 4
HALVES = 2
JH = J // HALVES
SCALAR_COLS = [256,96]


def interleave(copy, grouped, raw):
    copy(
        out=grouped.rearrange("p (c i) t -> p c t i", i=4),
        in_=raw.rearrange("p t (c i) -> p c t i", i=4),
    )


def quantise(nc, codes, scales, grouped):
    nc.vector.quantize_mx(out=codes.bitcast(FP8X4), scales=scales, in_=grouped.rearrange("p c t -> p (c t)"))


def tile_attend_gpcarrymix_kernel(tc, tab_words, tab_scales, w1, w2, bias, carry, wo, dy, og, base, offs, offs2, out):
    nc = tc.nc
    with ExitStack() as ctx:
        sb = ctx.enter_context(tc.tile_pool(name="sb", bufs=1))
        ps = ctx.enter_context(tc.psum_pool(name="ps", bufs=1))

        def tile(name, shape, dtype, tag=None):
            return sb.tile(shape, dtype, name=name, tag=tag or name, align_bytes=64)

        def scalar_cast(out, in_):
            nc.scalar.activation(out=out, in_=in_, func=ACT.Copy)

        offs_sb = tile("offs_sb", [P, J // 16], U16)
        offs2_sb = tile("offs2_sb", [P, J // 16], U16)
        words = tile("words", [P, T], U16)
        bytes_ = tile("scale_bytes", [P, T], U8)
        bias_sb = tile("bias_sb", [P, 1], F32)
        og_sb = tile("og_sb", [P, 1], F32)
        carry_sb = tile("carry_sb", [P, U], F32)
        raw = {n: tile(n + "_raw", [P, PACK, R], F32) for n in ("w2", "w1", "wo")}
        dy_raw = [tile("dy_raw%d" % h, [P, PACK, JH], F32) for h in range(HALVES)]
        base_sb = tile("base_sb", [P, J], F32)
        dy_v = dy.rearrange("(p t) j -> p t j", t=PACK)
        weights = {"w2": w2, "w1": w1, "wo": wo}

        def load(name, eng):
            if name == "scales":
                for q in range(4):
                    eng.dma_start(
                        out=bytes_[32 * q : 32 * q + 4, :].bitcast(I32),
                        in_=tab_scales[0, 4 * q : 4 * q + 4, :].bitcast(I32),
                    )
            elif name in weights:
                eng.dma_start(out=raw[name][:], in_=weights[name].rearrange("(p t) r -> p t r", t=PACK))
            elif name == "words":
                eng.dma_start(out=words[:].bitcast(I32), in_=tab_words[0].bitcast(I32))
            elif name in ("dy0", "dy1"):
                h = int(name[2])
                eng.dma_start(out=dy_raw[h][:], in_=dy_v[:, :, h * JH : (h + 1) * JH])
            else:
                dst, src = {"offs": (offs_sb, offs), "offs2": (offs2_sb, offs2), "bias": (bias_sb, bias), "og": (og_sb, og),
                            "carry": (carry_sb, carry), "base": (base_sb, base)}[name]
                eng.dma_start(dst[:], src)

        nc.vector.memset(bytes_[:].bitcast(I32)[:, :256], 0)
        nc.gpsimd.memset(bytes_[:].bitcast(I32)[:, 256:], 0)
        load("bias", nc.gpsimd)
        load("og", nc.gpsimd)
        load("offs", nc.sync)
        load("offs2", nc.sync)
        load("words", nc.sync)
        load("scales", nc.sync)
        load("w2", nc.sync)
        load("w1", nc.sync)
        load("carry", nc.sync)
        load("wo", nc.sync)
        load("dy0", nc.sync)
        load("dy1", nc.sync)
        load("base", nc.sync)

        g_bytes = tile("g_bytes", [P, J], U8)
        g_words = tile("g_words", [P, J], U16)

        pair_grouped = tile("pair_grouped", [P, 2 * R, PACK], BF16)
        pair_codes = tile("pair_codes", [P, 2 * R], U32)
        pair_scales = tile("pair_scales", [P, 2 * R], U8)
        grouped = {"wo": tile("wo_grouped", [P, R, PACK], BF16)}
        codes = {"wo": tile("wo_codes", [P, R], U32)}
        scales = {"wo": tile("wo_scales", [P, R], U8)}
        part = {"w2": slice(0, R), "w1": slice(R, 2 * R)}
        for n in part:
            interleave(scalar_cast, pair_grouped[:, part[n], :], raw[n][:])
        interleave(scalar_cast, grouped["wo"][:], raw["wo"][:])
        half_bias = tile("half_bias", [P, 1], F32)
        nc.gpsimd.tensor_scalar(half_bias[:], bias_sb[:], 0.5, 0.0, ALU.mult, ALU.add)

        cols = [slice(h * JH, (h + 1) * JH) for h in range(HALVES)]
        ocols = [slice(h * JH // 16, (h + 1) * JH // 16) for h in range(HALVES)]
        t = tile("t", [P, J], F32)
        h1 = tile("h1", [P, J], F32)
        t2 = tile("t2", [P, J], F32)
        d = tile("d", [P, J], F32)
        e = tile("e", [P, J], F32)

        nc.vector.tensor_copy(g_words[:], words[:].indirect(offs_sb[:]))
        nc.vector.tensor_copy(g_bytes[:], bytes_[:].indirect(offs_sb[:]))
        sums = {}
        quantise(nc, pair_codes[:], pair_scales[:], pair_grouped[:])
        for n in ("w2", "w1"):
            sums[n] = ps.tile([P, J], F32, name=n + "_sums")
            nc.tensor.matmul_mx(
                out=sums[n][:], lhsT=pair_codes[:, part[n]].bitcast(FP8X4), lhsT_scale=pair_scales[:, part[n]],
                rhs=g_words[:].bitcast(FP4X4), rhs_scale=g_bytes[:], start=True, stop=True,
            )
        nc.scalar.activation(out=t[:], in_=sums["w2"][:], func=ACT.Tanh, bias=half_bias[:], scale=0.5)
        nc.scalar.activation(out=h1[:], in_=sums["w1"][:], func=ACT.Tanh)
        nc.scalar.activation(out=t2[:], in_=t[:], func=ACT.Square)
        g_carry = tile("g_carry", [P, J], F32, tag="pair_grouped")
        nc.vector.tensor_copy(g_carry[:], carry_sb[:].indirect(offs2_sb[:]))
        quantise(nc, codes["wo"][:], scales["wo"][:], grouped["wo"][:])

        pieces = [(0, 0, 256, nc.vector.tensor_copy), (1, 0, 128, scalar_cast), (1, 128, 128, scalar_cast)]
        work = []
        for i, (h, c, w, copy) in enumerate(pieces):
            names = {"grouped": ([P, w, PACK], BF16), "codes": ([P, w], U32), "scales": ([P, w], U8),
                     "q": ([P, w], F32), "q2": ([P, w], F32), "r": ([P, w], F32), "y": ([P, w], F32)}
            x = {n: tile("dy_%s%d" % (n, i), *spec, tag="dy_raw1" if (n, i) == ("q2", 0) else None) for n, spec in names.items()}
            x["c0"] = ps.tile([P, w], F32, name="c0_%d" % i)
            x["cols"] = slice(h * JH + c, h * JH + c + w)
            x["copy"], x["raw"] = copy, dy_raw[h][:, :, c : c + w]
            work.append(x)

        def lay(x):
            interleave(x["copy"], x["grouped"][:], x["raw"])

        def product(x):
            quantise(nc, x["codes"][:], x["scales"][:], x["grouped"][:])
            nc.tensor.matmul_mx(
                out=x["c0"][:], lhsT=codes["wo"][:].bitcast(FP8X4), lhsT_scale=scales["wo"][:],
                rhs=x["codes"][:].bitcast(FP8X4), rhs_scale=x["scales"][:], start=True, stop=True,
            )

        def square(x):
            nc.vector.tensor_tensor(x["q"][:], x["c0"][:], e[:, x["cols"]], ALU.mult)
            nc.scalar.activation(out=x["q2"][:], in_=x["q"][:], func=ACT.Square, scale=math.sqrt(0.125))

        def gain(x):
            nc.vector.scalar_tensor_tensor(x["r"][:], x["q2"][:], og_sb[:], t[:, x["cols"]], ALU.mult, ALU.mult)

        def finish(x):
            nc.vector.tensor_tensor(x["y"][:], base_sb[:, x["cols"]], x["r"][:], ALU.subtract)
            nc.sync.dma_start(out=out[:, x["cols"]], in_=x["y"][:])

        lay(work[0])
        product(work[0])
        nc.vector.tensor_tensor(d[:], h1[:], g_carry[:], ALU.subtract)
        nc.vector.scalar_tensor_tensor(e[:], t2[:], 1.0, d[:], ALU.subtract, ALU.mult)
        for x in work[1:]:
            lay(x)
        for x in work[1:]:
            product(x)
        for x in work:
            square(x)
        for x in work:
            gain(x)
            finish(x)
